import numpy as np
import ml_dtypes


def mxq(x, axis, fmt="e4m3"):
    dtype, down = {"e4m3": (ml_dtypes.float8_e4m3fn, 7), "e5m2": (ml_dtypes.float8_e5m2, 14)}[fmt]
    v = np.moveaxis(np.asarray(x, np.float32).astype(ml_dtypes.bfloat16).astype(np.float64), axis, -1)
    blocks = v.reshape(v.shape[:-1] + (-1, 32))
    amax = np.abs(blocks).max(-1, keepdims=True)
    byte = np.maximum(np.where(amax > 0, np.frexp(amax)[1] - 1 + 127, 0) - down, 1)
    scale = np.exp2(byte - 127.0)
    codes = (blocks / scale).astype(np.float32).astype(dtype).astype(np.float64)
    return np.moveaxis((codes * scale).reshape(v.shape), -1, axis)


WIDE = False


def mx_kscale(k):
    if not WIDE:
        return np.ones(k)
    levels = np.array([30, -30])
    if k % 512:
        return np.exp2(np.random.permutation(np.resize(levels, k // 32))).repeat(32)
    a = np.empty((k // 512, 16))
    for p in range(k // 512):
        a[p, :8] = np.random.permutation(np.resize(levels, 8))
        for g in range(8):
            far = levels[np.abs(levels - a[p, g]) >= 10]
            a[p, g + 8] = far[np.random.randint(len(far))]
    return np.exp2(a.ravel()).repeat(32)


def f64(x):
    return np.asarray(x).astype(np.float64)


def striped(idx):
    return np.tile(np.asarray(idx).reshape(-1, 16).T, (8, 1)).astype(np.uint16)


def unstriped(offs):
    return offs[:16].T.reshape(-1).astype(np.int64)


E2M1 = np.array([0.0, 0.5, 1.0, 1.5, 2.0, 3.0, 4.0, 6.0, -0.0, -0.5, -1.0, -1.5, -2.0, -3.0, -4.0, -6.0])


def pack_weight(w, fmt):
    k, n = w.shape
    w = f64(np.asarray(w, np.float32).astype(ml_dtypes.bfloat16)).reshape(k // 32, 32, n)
    amax = np.abs(w).max(1)
    if fmt in ("e4m3", "e5m2"):
        byte = np.frexp(amax)[1] - 1 + 127 - (7 if fmt == "e4m3" else 14)
    else:
        mant, ex = np.frexp(amax / 6.0)
        byte = np.where(mant > 0.5, ex, ex - 1) + 127
    byte = np.clip(np.where(amax > 0, byte, 1), 1, 254)
    scaled = (w * np.exp2(127.0 - byte)[:, None, :]).reshape(k, n).astype(np.float32)
    by_word = np.ascontiguousarray(scaled.reshape(k // 512, 128, 4, n).transpose(0, 1, 3, 2))
    if fmt in ("e4m3", "e5m2"):
        words = by_word.astype(ml_dtypes.float8_e4m3fn if fmt == "e4m3" else ml_dtypes.float8_e5m2).view(np.uint8)
    else:
        c = by_word.astype(ml_dtypes.float4_e2m1fn).view(np.uint8) & 0xF
        words = (c[..., 0::2] | (c[..., 1::2] << 4)).reshape(k // 512, 128, 2 * n)
    return np.ascontiguousarray(words), np.ascontiguousarray(byte.astype(np.uint8).reshape(k // 512, 16, n))


def unpack_weight(words, scales, fmt):
    g, _, n = scales.shape
    words = np.ascontiguousarray(words).reshape(g, 128, n, -1)
    if fmt in ("e4m3", "e5m2"):
        vals = words.view(ml_dtypes.float8_e4m3fn if fmt == "e4m3" else ml_dtypes.float8_e5m2).astype(np.float64)
    else:
        nib = np.empty((g, 128, n, 4), np.uint8)
        nib[..., 0::2] = words & 0xF
        nib[..., 1::2] = words >> 4
        vals = E2M1[nib]
    vals = vals * np.repeat(np.exp2(scales.astype(np.float64) - 127.0), 8, axis=1)[..., None]
    return vals.transpose(0, 1, 3, 2).reshape(g * 512, n)


def sigmoid(v):
    return 1.0 / (1.0 + np.exp(-v))


K, F, T, Z, J, R, O, N, E = 512, 512, 1024, 1024, 256, 512, 128, 256, 1024


def setup_inputs():
    n = np.random.standard_normal
    idx = np.random.permutation(T)[:J]
    idx2 = np.random.permutation(Z)[:J]
    idx3 = np.random.permutation(J)[:O]
    idx4 = np.random.permutation(J)[:O]
    idx5 = np.random.permutation(E)[:O]
    fk = mx_kscale(K)
    ff = mx_kscale(F)
    fr = mx_kscale(R)
    xtp = pack_weight(n((K, T)) / fk[:, None], "e4m3")
    wp = pack_weight(n((K, R)) * 1 / np.sqrt(K) * fk[:, None], "e2m1")
    xop = pack_weight(n((F, Z)) / ff[:, None], "e2m1")
    w2p = pack_weight(n((F, R)) * 1 / np.sqrt(F) * ff[:, None] * fr, "e5m2")
    wbp = pack_weight(n((R, N)) * 1 / np.sqrt(R) / fr[:, None], "e5m2")
    return {
        "xt_words": xtp[0],
        "xt_scales": xtp[1],
        "w_words": wp[0],
        "w_scales": wp[1],
        "xo_words": xop[0],
        "xo_scales": xop[1],
        "w2_words": w2p[0],
        "w2_scales": w2p[1],
        "sg": (np.random.uniform(0.6, 1.6, (R, 1))).astype(np.float32),
        "wb_words": wbp[0],
        "wb_scales": wbp[1],
        "tz": (n((N, E))).astype(np.float32),
        "offs": striped(idx),
        "offs2": striped(idx2),
        "offs3": striped(idx3),
        "offs4": striped(idx4),
        "offs5": striped(idx5),
    }


def reference(xt_words, xt_scales, w_words, w_scales, xo_words, xo_scales, w2_words, w2_scales, sg, wb_words, wb_scales, tz, offs, offs2, offs3, offs4, offs5):
    idx = unstriped(offs)
    idx2 = unstriped(offs2)
    idx3 = unstriped(offs3)
    idx4 = unstriped(offs4)
    idx5 = unstriped(offs5)
    xtu = unpack_weight(xt_words, xt_scales, "e4m3")
    wu = unpack_weight(w_words, w_scales, "e2m1")
    xou = unpack_weight(xo_words, xo_scales, "e2m1")
    w2u = unpack_weight(w2_words, w2_scales, "e5m2")
    wbu = unpack_weight(wb_words, wb_scales, "e5m2")
    xtidxg = xtu[:, idx]
    a = wu.T @ xtidxg
    xoidx2g = xou[:, idx2]
    b = w2u.T @ xoidx2g
    hid = np.maximum(b[:, idx3], b[:, idx4]) * sigmoid(a[:, idx4] * f64(sg))
    hidq = mxq(hid, 0, "e4m3")
    p = wbu.T @ hidq
    y = p + f64(tz)[:, idx5]
    return y

@@ -1,0 +1,180 @@
+from contextlib import ExitStack
+
+import concourse.mybir as mybir
+
+K, F, T, Z, J, R, O, N, E = 512, 512, 1024, 1024, 256, 512, 128, 256, 1024
+FLOPS = 2 * (K * R * J + F * R * J + R * N * O)
+
+F32 = mybir.dt.float32
+BF16 = mybir.dt.bfloat16
+I32 = mybir.dt.int32
+U32 = mybir.dt.uint32
+U16 = mybir.dt.uint16
+U8 = mybir.dt.uint8
+E4M3 = mybir.dt.float8_e4m3fn_x4
+E5M2 = mybir.dt.float8_e5m2_x4
+E2M1 = mybir.dt.float4_e2m1fn_x4
+ACT = mybir.ActivationFunctionType
+ALU = mybir.AluOpType
+
+P = 128
+PACK = 4
+QUADS = 4
+LINE = 16
+
+
+def load_scale_rows(queue, plane, scales):
+    for q in range(QUADS):
+        queue.dma_start(
+            out=plane[32 * q : 32 * q + 4, :].bitcast(I32),
+            in_=scales[0, 4 * q : 4 * q + 4, :].bitcast(I32),
+        )
+
+
+def deal_columns(copy, dealt, given, run):
+    copy(
+        out=dealt.rearrange("p (t c i) -> p c t i", t=PACK, i=run),
+        in_=given.rearrange("p (c i t) -> p c t i", t=PACK, i=run),
+    )
+
+
+def tile_list_twotab_agree_one_tabled_kernel(
+    tc, xt_words, xt_scales, w_words, w_scales, xo_words, xo_scales, w2_words, w2_scales,
+    sg, wb_words, wb_scales, tz, offs, offs2, offs3, offs4, offs5, out,
+):
+    nc = tc.nc
+    with ExitStack() as ctx:
+        sb = ctx.enter_context(tc.tile_pool(name="sb", bufs=1))
+        psum = ctx.enter_context(tc.psum_pool(name="psum", bufs=1))
+
+        def tile(name, shape, dtype):
+            return sb.tile(shape, dtype, name=name, align_bytes=64)
+
+        token_list = tile("token_list", [P, J // 16], U16)
+        note_list = tile("note_list", [P, J // 16], U16)
+        first_list = tile("first_list", [P, O // 16], U16)
+        second_list = tile("second_list", [P, O // 16], U16)
+        entry_list = tile("entry_list", [P, O // 16], U16)
+
+        xo_w = tile("xo_w", [P, Z], U16)
+        xo_s = tile("xo_s", [P, Z], U8)
+        w2_w = tile("w2_w", [P, R], U32)
+        w2_s = tile("w2_s", [P, R], U8)
+        xt_w = tile("xt_w", [P, T], U32)
+        xt_s = tile("xt_s", [P, T], U8)
+        w_w = tile("w_w", [P, R], U16)
+        w_s = tile("w_s", [P, R], U8)
+        wb_w = tile("wb_w", [P, N], U32)
+        wb_s = tile("wb_s", [P, N], U8)
+        slope = tile("slope", [P, PACK], F32)
+        tz_rows = tile("tz_rows", [P, N // P, E], F32)
+
+        for plane in (xt_s, w_s):
+            nc.gpsimd.memset(plane[:].bitcast(I32), 0)
+        for plane in (xo_s, w2_s, wb_s):
+            nc.vector.memset(plane[:].bitcast(I32), 0)
+
+        load_scale_rows(nc.sync, xt_s, xt_scales)
+        nc.sync.dma_start(token_list[:], offs)
+        nc.sync.dma_start(out=xt_w[:].bitcast(I32), in_=xt_words[0].rearrange("p n t -> p (n t)").bitcast(I32))
+        nc.sync.dma_start(out=w_w[:].bitcast(I32), in_=w_words[0].bitcast(I32))
+        nc.sync.dma_start(out=w2_w[:].bitcast(I32), in_=w2_words[0].rearrange("p n t -> p (n t)").bitcast(I32))
+        load_scale_rows(nc.sync, w_s, w_scales)
+        nc.sync.dma_start(note_list[:], offs2)
+        nc.sync.dma_start(out=xo_w[:].bitcast(I32), in_=xo_words[0].bitcast(I32))
+        load_scale_rows(nc.sync, xo_s, xo_scales)
+        load_scale_rows(nc.sync, w2_s, w2_scales)
+        nc.sync.dma_start(second_list[:], offs4)
+        nc.sync.dma_start(out=slope[:], in_=sg.rearrange("(p t) o -> p (t o)", t=PACK))
+        nc.sync.dma_start(first_list[:], offs3)
+        nc.sync.dma_start(out=wb_w[:].bitcast(I32), in_=wb_words[0].rearrange("p n t -> p (n t)").bitcast(I32))
+        load_scale_rows(nc.sync, wb_s, wb_scales)
+        nc.sync.dma_start(entry_list[:], offs5)
+        nc.sync.dma_start(out=tz_rows[:], in_=tz.rearrange("(h p) e -> p h e", p=P))
+
+        xt_gw = tile("xt_gw", [P, J], U32)
+        xt_gs = tile("xt_gs", [P, J], U8)
+        w_dw = tile("w_dw", [P, R], U16)
+        w_ds = tile("w_ds", [P, R], U8)
+        nc.vector.tensor_copy(xt_gs[:], xt_s[:].indirect(token_list[:]))
+        nc.vector.tensor_copy(xt_gw[:], xt_w[:].indirect(token_list[:]))
+        deal_columns(nc.scalar.copy, w_dw[:], w_w[:], LINE // 2)
+        deal_columns(nc.vector.tensor_copy, w_ds[:], w_s[:], LINE)
+
+        xo_gw = tile("xo_gw", [P, J], U16)
+        xo_gs = tile("xo_gs", [P, J], U8)
+        w2_dw = tile("w2_dw", [P, R], U32)
+        w2_ds = tile("w2_ds", [P, R], U8)
+        deal_columns(nc.scalar.copy, w2_dw[:], w2_w[:], LINE // 4)
+        nc.vector.tensor_copy(xo_gw[:], xo_w[:].indirect(note_list[:]))
+        nc.vector.tensor_copy(xo_gs[:], xo_s[:].indirect(note_list[:]))
+        deal_columns(nc.vector.tensor_copy, w2_ds[:], w2_s[:], LINE)
+
+        a_banks = [psum.tile([P, J], F32, name=f"a_bank{t}") for t in range(PACK)]
+        for t in range(PACK):
+            cols = slice(t * P, (t + 1) * P)
+            nc.tensor.matmul_mx(
+                out=a_banks[t][:], lhsT=w_dw[:, cols].bitcast(E2M1), lhsT_scale=w_ds[:, cols],
+                rhs=xt_gw[:].bitcast(E4M3), rhs_scale=xt_gs[:], start=True, stop=True,
+            )
+        b_banks = [psum.tile([P, J], F32, name=f"b_bank{t}") for t in range(PACK)]
+        for t in range(PACK):
+            cols = slice(t * P, (t + 1) * P)
+            nc.tensor.matmul_mx(
+                out=b_banks[t][:], lhsT=w2_dw[:, cols].bitcast(E5M2), lhsT_scale=w2_ds[:, cols],
+                rhs=xo_gw[:].bitcast(E2M1), rhs_scale=xo_gs[:], start=True, stop=True,
+            )
+
+        a_rows = [tile(f"a_rows{t}", [P, J], F32) for t in range(PACK)]
+        gate = tile("gate", [P, PACK, O], F32)
+        for t in range(PACK):
+            nc.scalar.copy(out=a_rows[t][:], in_=a_banks[t][:])
+            nc.scalar.activation(
+                out=gate[:, t, :], in_=a_rows[t][:].indirect(second_list[:]),
+                func=ACT.Sigmoid, scale=slope[:, t : t + 1],
+            )
+
+        b_rows = [tile(f"b_rows{t}", [P, J], F32) for t in range(PACK)]
+        b_first = tile("b_first", [P, PACK, O], F32)
+        b_second = tile("b_second", [P, PACK, O], F32)
+        larger = tile("larger", [P, PACK, O], F32)
+        for t in (0, 1):
+            nc.vector.tensor_copy(out=b_rows[t][:], in_=b_banks[t][:])
+        for t in (2, 3):
+            nc.scalar.copy(out=b_rows[t][:], in_=b_banks[t][:])
+        for t in (0, 1):
+            nc.vector.tensor_copy(b_first[:, t, :], b_rows[t][:].indirect(first_list[:]))
+            nc.vector.tensor_copy(b_second[:, t, :], b_rows[t][:].indirect(second_list[:]))
+        nc.vector.tensor_copy(b_first[:, 2, :], b_rows[2][:].indirect(first_list[:]))
+        nc.scalar.activation(out=b_second[:, 2, :], in_=b_rows[2][:].indirect(second_list[:]), func=ACT.Copy)
+        nc.scalar.activation(out=b_first[:, 3, :], in_=b_rows[3][:].indirect(first_list[:]), func=ACT.Copy)
+        nc.scalar.activation(out=b_second[:, 3, :], in_=b_rows[3][:].indirect(second_list[:]), func=ACT.Copy)
+        for pair in (slice(0, 2), slice(2, 4)):
+            nc.vector.tensor_tensor(out=larger[:, pair, :], in0=b_first[:, pair, :], in1=b_second[:, pair, :], op=ALU.max)
+
+
+        hid = tile("hid", [P, O * PACK], BF16)
+        nc.vector.tensor_tensor(
+            out=hid[:].rearrange("p (c i t) -> p c t i", t=PACK, i=4),
+            in0=larger[:].rearrange("p t (c i) -> p c t i", i=4),
+            in1=gate[:].rearrange("p t (c i) -> p c t i", i=4),
+            op=ALU.mult,
+        )
+        hid_w = tile("hid_w", [P, O], U32)
+        hid_s = tile("hid_s", [P, O], U8)
+        nc.vector.quantize_mx(out=hid_w[:].bitcast(E4M3), scales=hid_s[:], in_=hid[:])
+
+        tz_picked = tile("tz_picked", [P, N // P, O], F32)
+        for h in range(N // P):
+            nc.scalar.activation(out=tz_picked[:, h, :], in_=tz_rows[:, h, :].indirect(entry_list[:]), func=ACT.Copy)
+
+        p_bank = psum.tile([P, N // P, O], F32, name="a_bank0")
+        for h in range(N // P):
+            cols = slice(h * P, (h + 1) * P)
+            nc.tensor.matmul_mx(
+                out=p_bank[:, h, :], lhsT=wb_w[:, cols].bitcast(E5M2), lhsT_scale=wb_s[:, cols],
+                rhs=hid_w[:].bitcast(E4M3), rhs_scale=hid_s[:], start=True, stop=True,
+            )
+        result = tile("result", [P, N // P, O], F32)
+        nc.vector.tensor_tensor(out=result[:], in0=p_bank[:], in1=tz_picked[:], op=ALU.add)
+        nc.sync.dma_start(out=out.rearrange("(h p) o -> p h o", p=P), in_=result[:])

@@ -23,12 +23,13 @@ QUADS = 4
 LINE = 16
 
 
-def load_scale_rows(queue, plane, scales):
-    for q in range(QUADS):
-        queue.dma_start(
-            out=plane[32 * q : 32 * q + 4, :].bitcast(I32),
-            in_=scales[0, 4 * q : 4 * q + 4, :].bitcast(I32),
-        )
+def load_low_rows(queue, plane, scales):
+    queue.dma_start(out=plane[0:16, :].bitcast(I32), in_=scales[0].bitcast(I32))
+
+
+def load_high_rows(queue, plane, scales):
+    rows = scales[0, 2:16, :].bitcast(I32)
+    queue.dma_start(out=plane[16:P, :].bitcast(I32), in_=rows.unsqueeze(0).broadcast_to([8, 14, rows.shape[1]]))
 
 
 def deal_columns(copy, dealt, given, run):
@@ -36,6 +37,10 @@ def deal_columns(copy, dealt, given, run):
         out=dealt.rearrange("p (t c i) -> p c t i", t=PACK, i=run),
         in_=given.rearrange("p (c i t) -> p c t i", t=PACK, i=run),
     )
+
+
+def deal_slot(copy, dealt, given, t):
+    copy(out=dealt[:, t * P : (t + 1) * P], in_=given[:, t :: PACK])
 
 
 def tile_list_twotab_agree_one_tabled_kernel(
@@ -69,54 +74,54 @@ def tile_list_twotab_agree_one_tabled_kernel(
         slope = tile("slope", [P, PACK], F32)
         tz_rows = tile("tz_rows", [P, N // P, E], F32)
 
-        for plane in (xt_s, w_s):
-            nc.gpsimd.memset(plane[:].bitcast(I32), 0)
-        for plane in (xo_s, w2_s, wb_s):
-            nc.vector.memset(plane[:].bitcast(I32), 0)
 
-        load_scale_rows(nc.sync, xt_s, xt_scales)
-        nc.sync.dma_start(token_list[:], offs)
-        nc.sync.dma_start(out=xt_w[:].bitcast(I32), in_=xt_words[0].rearrange("p n t -> p (n t)").bitcast(I32))
-        nc.sync.dma_start(out=w_w[:].bitcast(I32), in_=w_words[0].bitcast(I32))
-        nc.sync.dma_start(out=w2_w[:].bitcast(I32), in_=w2_words[0].rearrange("p n t -> p (n t)").bitcast(I32))
-        load_scale_rows(nc.sync, w_s, w_scales)
+        load_high_rows(nc.scalar, xo_s, xo_scales)
+        nc.gpsimd.dma_start(out=w_w[:].bitcast(I32), in_=w_words[0].bitcast(I32))
+        load_high_rows(nc.gpsimd, xt_s, xt_scales)
+        load_high_rows(nc.gpsimd, w_s, w_scales)
+        load_high_rows(nc.gpsimd, wb_s, wb_scales)
         nc.sync.dma_start(note_list[:], offs2)
         nc.sync.dma_start(out=xo_w[:].bitcast(I32), in_=xo_words[0].bitcast(I32))
-        load_scale_rows(nc.sync, xo_s, xo_scales)
-        load_scale_rows(nc.sync, w2_s, w2_scales)
+        load_low_rows(nc.sync, xo_s, xo_scales)
+        load_low_rows(nc.sync, w2_s, w2_scales)
+        nc.sync.dma_start(out=w2_w[:].bitcast(I32), in_=w2_words[0].rearrange("p n t -> p (n t)").bitcast(I32))
+        load_high_rows(nc.sync, w2_s, w2_scales)
+        nc.sync.dma_start(out=xt_w[:].bitcast(I32), in_=xt_words[0].rearrange("p n t -> p (n t)").bitcast(I32))
+        nc.sync.dma_start(token_list[:], offs)
+        load_low_rows(nc.sync, xt_s, xt_scales)
+        load_low_rows(nc.sync, w_s, w_scales)
         nc.sync.dma_start(second_list[:], offs4)
-        nc.sync.dma_start(out=slope[:], in_=sg.rearrange("(p t) o -> p (t o)", t=PACK))
         nc.sync.dma_start(first_list[:], offs3)
+        nc.sync.dma_start(out=slope[:], in_=sg.rearrange("(p t) o -> p (t o)", t=PACK))
         nc.sync.dma_start(out=wb_w[:].bitcast(I32), in_=wb_words[0].rearrange("p n t -> p (n t)").bitcast(I32))
-        load_scale_rows(nc.sync, wb_s, wb_scales)
+        load_low_rows(nc.sync, wb_s, wb_scales)
         nc.sync.dma_start(entry_list[:], offs5)
         nc.sync.dma_start(out=tz_rows[:], in_=tz.rearrange("(h p) e -> p h e", p=P))
 
-        xt_gw = tile("xt_gw", [P, J], U32)
-        xt_gs = tile("xt_gs", [P, J], U8)
-        w_dw = tile("w_dw", [P, R], U16)
-        w_ds = tile("w_ds", [P, R], U8)
-        nc.vector.tensor_copy(xt_gs[:], xt_s[:].indirect(token_list[:]))
-        nc.vector.tensor_copy(xt_gw[:], xt_w[:].indirect(token_list[:]))
-        deal_columns(nc.scalar.copy, w_dw[:], w_w[:], LINE // 2)
-        deal_columns(nc.vector.tensor_copy, w_ds[:], w_s[:], LINE)
+        idle = tile("idle", [P, 2], F32)
+        nc.vector.memset(idle[:, 0:1], 0.0)
+        nc.scalar.activation(out=idle[:, 1:2], in_=idle[:, 0:1], func=ACT.Sigmoid)
 
         xo_gw = tile("xo_gw", [P, J], U16)
         xo_gs = tile("xo_gs", [P, J], U8)
         w2_dw = tile("w2_dw", [P, R], U32)
         w2_ds = tile("w2_ds", [P, R], U8)
-        deal_columns(nc.scalar.copy, w2_dw[:], w2_w[:], LINE // 4)
         nc.vector.tensor_copy(xo_gw[:], xo_w[:].indirect(note_list[:]))
         nc.vector.tensor_copy(xo_gs[:], xo_s[:].indirect(note_list[:]))
-        deal_columns(nc.vector.tensor_copy, w2_ds[:], w2_s[:], LINE)
-
-        a_banks = [psum.tile([P, J], F32, name=f"a_bank{t}") for t in range(PACK)]
+        deal_columns(nc.scalar.copy, w2_dw[:], w2_w[:], LINE // 4)
         for t in range(PACK):
-            cols = slice(t * P, (t + 1) * P)
-            nc.tensor.matmul_mx(
-                out=a_banks[t][:], lhsT=w_dw[:, cols].bitcast(E2M1), lhsT_scale=w_ds[:, cols],
-                rhs=xt_gw[:].bitcast(E4M3), rhs_scale=xt_gs[:], start=True, stop=True,
-            )
+            deal_slot(nc.vector.tensor_copy, w2_ds, w2_s, t)
+
+        xt_gw = tile("xt_gw", [P, J], U32)
+        xt_gs = tile("xt_gs", [P, J], U8)
+        w_dw = tile("w2_w", [P, R], U16)
+        w_ds = tile("w_ds", [P, R], U8)
+        deal_columns(nc.scalar.copy, w_dw[:], w_w[:], LINE // 2)
+        nc.vector.tensor_copy(xt_gw[:], xt_w[:].indirect(token_list[:]))
+        nc.vector.tensor_copy(xt_gs[:], xt_s[:].indirect(token_list[:]))
+        for t in range(PACK):
+            deal_slot(nc.vector.tensor_copy, w_ds, w_s, t)
+
         b_banks = [psum.tile([P, J], F32, name=f"b_bank{t}") for t in range(PACK)]
         for t in range(PACK):
             cols = slice(t * P, (t + 1) * P)
@@ -124,34 +129,35 @@ def tile_list_twotab_agree_one_tabled_kernel(
                 out=b_banks[t][:], lhsT=w2_dw[:, cols].bitcast(E5M2), lhsT_scale=w2_ds[:, cols],
                 rhs=xo_gw[:].bitcast(E2M1), rhs_scale=xo_gs[:], start=True, stop=True,
             )
+        a_banks = [psum.tile([P, J], F32, name=f"a_bank{t}") for t in range(PACK)]
+        for t in range(PACK):
+            cols = slice(t * P, (t + 1) * P)
+            nc.tensor.matmul_mx(
+                out=a_banks[t][:], lhsT=w_dw[:, cols].bitcast(E2M1), lhsT_scale=w_ds[:, cols],
+                rhs=xt_gw[:].bitcast(E4M3), rhs_scale=xt_gs[:], start=True, stop=True,
+            )
 
         a_rows = [tile(f"a_rows{t}", [P, J], F32) for t in range(PACK)]
+        b_rows = [tile(f"b_rows{t}", [P, J], F32) for t in range(PACK)]
+        b_first = tile("b_first", [P, PACK, O], F32)
+        b_second = tile("b_second", [P, PACK, O], F32)
         gate = tile("gate", [P, PACK, O], F32)
+        larger = tile("larger", [P, PACK, O], F32)
         for t in range(PACK):
-            nc.scalar.copy(out=a_rows[t][:], in_=a_banks[t][:])
+            nc.scalar.copy(out=b_rows[t][:], in_=b_banks[t][:])
+        nc.scalar.activation(out=b_first[:, 0, :], in_=b_rows[0][:].indirect(first_list[:]), func=ACT.Copy)
+        for t in range(PACK):
+            nc.scalar.activation(out=b_second[:, t, :], in_=b_rows[t][:].indirect(second_list[:]), func=ACT.Copy)
+        for t in range(PACK):
+            if t > 0:
+                nc.vector.tensor_copy(b_first[:, t, :], b_rows[t][:].indirect(first_list[:]))
+            nc.vector.tensor_copy(out=a_rows[t][:], in_=a_banks[t][:])
+        for t in range(PACK):
             nc.scalar.activation(
                 out=gate[:, t, :], in_=a_rows[t][:].indirect(second_list[:]),
                 func=ACT.Sigmoid, scale=slope[:, t : t + 1],
             )
-
-        b_rows = [tile(f"b_rows{t}", [P, J], F32) for t in range(PACK)]
-        b_first = tile("b_first", [P, PACK, O], F32)
-        b_second = tile("b_second", [P, PACK, O], F32)
-        larger = tile("larger", [P, PACK, O], F32)
-        for t in (0, 1):
-            nc.vector.tensor_copy(out=b_rows[t][:], in_=b_banks[t][:])
-        for t in (2, 3):
-            nc.scalar.copy(out=b_rows[t][:], in_=b_banks[t][:])
-        for t in (0, 1):
-            nc.vector.tensor_copy(b_first[:, t, :], b_rows[t][:].indirect(first_list[:]))
-            nc.vector.tensor_copy(b_second[:, t, :], b_rows[t][:].indirect(second_list[:]))
-        nc.vector.tensor_copy(b_first[:, 2, :], b_rows[2][:].indirect(first_list[:]))
-        nc.scalar.activation(out=b_second[:, 2, :], in_=b_rows[2][:].indirect(second_list[:]), func=ACT.Copy)
-        nc.scalar.activation(out=b_first[:, 3, :], in_=b_rows[3][:].indirect(first_list[:]), func=ACT.Copy)
-        nc.scalar.activation(out=b_second[:, 3, :], in_=b_rows[3][:].indirect(second_list[:]), func=ACT.Copy)
-        for pair in (slice(0, 2), slice(2, 4)):
-            nc.vector.tensor_tensor(out=larger[:, pair, :], in0=b_first[:, pair, :], in1=b_second[:, pair, :], op=ALU.max)
-
+        nc.vector.tensor_tensor(out=larger[:], in0=b_first[:], in1=b_second[:], op=ALU.max)
 
         hid = tile("hid", [P, O * PACK], BF16)
         nc.vector.tensor_tensor(
@@ -164,17 +170,17 @@ def tile_list_twotab_agree_one_tabled_kernel(
         hid_s = tile("hid_s", [P, O], U8)
         nc.vector.quantize_mx(out=hid_w[:].bitcast(E4M3), scales=hid_s[:], in_=hid[:])
 
-        tz_picked = tile("tz_picked", [P, N // P, O], F32)
+        tz_picked = tile("a_rows3", [P, N // P, O], F32)
         for h in range(N // P):
             nc.scalar.activation(out=tz_picked[:, h, :], in_=tz_rows[:, h, :].indirect(entry_list[:]), func=ACT.Copy)
 
-        p_bank = psum.tile([P, N // P, O], F32, name="a_bank0")
         for h in range(N // P):
             cols = slice(h * P, (h + 1) * P)
+            p_bank = psum.tile([P, O], F32, name=f"b_bank{h}")
             nc.tensor.matmul_mx(
-                out=p_bank[:, h, :], lhsT=wb_w[:, cols].bitcast(E5M2), lhsT_scale=wb_s[:, cols],
+                out=p_bank[:], lhsT=wb_w[:, cols].bitcast(E5M2), lhsT_scale=wb_s[:, cols],
                 rhs=hid_w[:].bitcast(E4M3), rhs_scale=hid_s[:], start=True, stop=True,
             )
-        result = tile("result", [P, N // P, O], F32)
-        nc.vector.tensor_tensor(out=result[:], in0=p_bank[:], in1=tz_picked[:], op=ALU.add)
-        nc.sync.dma_start(out=out.rearrange("(h p) o -> p h o", p=P), in_=result[:])
+            result = tile(f"result{h}", [P, O], F32)
+            nc.vector.tensor_tensor(out=result[:], in0=p_bank[:], in1=tz_picked[:, h, :], op=ALU.add)
+            nc.sync.dma_start(out=out[cols, :], in_=result[:])

@@ -76,7 +76,6 @@ def tile_list_twotab_agree_one_tabled_kernel(
 
 
         load_high_rows(nc.scalar, xo_s, xo_scales)
-        nc.gpsimd.dma_start(out=w_w[:].bitcast(I32), in_=w_words[0].bitcast(I32))
         load_high_rows(nc.gpsimd, xt_s, xt_scales)
         load_high_rows(nc.gpsimd, w_s, w_scales)
         load_high_rows(nc.gpsimd, wb_s, wb_scales)
@@ -85,12 +84,13 @@ def tile_list_twotab_agree_one_tabled_kernel(
         load_low_rows(nc.sync, xo_s, xo_scales)
         load_low_rows(nc.sync, w2_s, w2_scales)
         nc.sync.dma_start(out=w2_w[:].bitcast(I32), in_=w2_words[0].rearrange("p n t -> p (n t)").bitcast(I32))
+        nc.sync.dma_start(out=w_w[:].bitcast(I32), in_=w_words[0].bitcast(I32))
         load_high_rows(nc.sync, w2_s, w2_scales)
-        nc.sync.dma_start(out=xt_w[:].bitcast(I32), in_=xt_words[0].rearrange("p n t -> p (n t)").bitcast(I32))
         nc.sync.dma_start(token_list[:], offs)
         load_low_rows(nc.sync, xt_s, xt_scales)
         load_low_rows(nc.sync, w_s, w_scales)
         nc.sync.dma_start(second_list[:], offs4)
+        nc.sync.dma_start(out=xt_w[:].bitcast(I32), in_=xt_words[0].rearrange("p n t -> p (n t)").bitcast(I32))
         nc.sync.dma_start(first_list[:], offs3)
         nc.sync.dma_start(out=slope[:], in_=sg.rearrange("(p t) o -> p (t o)", t=PACK))
         nc.sync.dma_start(out=wb_w[:].bitcast(I32), in_=wb_words[0].rearrange("p n t -> p (n t)").bitcast(I32))
@@ -117,10 +117,10 @@ def tile_list_twotab_agree_one_tabled_kernel(
         w_dw = tile("w2_w", [P, R], U16)
         w_ds = tile("w_ds", [P, R], U8)
         deal_columns(nc.scalar.copy, w_dw[:], w_w[:], LINE // 2)
-        nc.vector.tensor_copy(xt_gw[:], xt_w[:].indirect(token_list[:]))
         nc.vector.tensor_copy(xt_gs[:], xt_s[:].indirect(token_list[:]))
         for t in range(PACK):
             deal_slot(nc.vector.tensor_copy, w_ds, w_s, t)
+        nc.vector.tensor_copy(xt_gw[:], xt_w[:].indirect(token_list[:]))
 
         b_banks = [psum.tile([P, J], F32, name=f"b_bank{t}") for t in range(PACK)]
         for t in range(PACK):
@@ -145,9 +145,9 @@ def tile_list_twotab_agree_one_tabled_kernel(
         larger = tile("larger", [P, PACK, O], F32)
         for t in range(PACK):
             nc.scalar.copy(out=b_rows[t][:], in_=b_banks[t][:])
-        nc.scalar.activation(out=b_first[:, 0, :], in_=b_rows[0][:].indirect(first_list[:]), func=ACT.Copy)
         for t in range(PACK):
             nc.scalar.activation(out=b_second[:, t, :], in_=b_rows[t][:].indirect(second_list[:]), func=ACT.Copy)
+        nc.scalar.activation(out=b_first[:, 0, :], in_=b_rows[0][:].indirect(first_list[:]), func=ACT.Copy)
         for t in range(PACK):
             if t > 0:
                 nc.vector.tensor_copy(b_first[:, t, :], b_rows[t][:].indirect(first_list[:]))

from contextlib import ExitStack

import concourse.mybir as mybir

K, F, T, Z, J, R, O, N, E = 512, 512, 1024, 1024, 256, 512, 128, 256, 1024
FLOPS = 2 * (K * R * J + F * R * J + R * N * O)

F32 = mybir.dt.float32
BF16 = mybir.dt.bfloat16
I32 = mybir.dt.int32
U32 = mybir.dt.uint32
U16 = mybir.dt.uint16
U8 = mybir.dt.uint8
E4M3 = mybir.dt.float8_e4m3fn_x4
E5M2 = mybir.dt.float8_e5m2_x4
E2M1 = mybir.dt.float4_e2m1fn_x4
ACT = mybir.ActivationFunctionType
ALU = mybir.AluOpType

P = 128
PACK = 4
QUADS = 4
LINE = 16


def load_low_rows(queue, plane, scales):
    queue.dma_start(out=plane[0:16, :].bitcast(I32), in_=scales[0].bitcast(I32))


def load_high_rows(queue, plane, scales):
    rows = scales[0, 2:16, :].bitcast(I32)
    queue.dma_start(out=plane[16:P, :].bitcast(I32), in_=rows.unsqueeze(0).broadcast_to([8, 14, rows.shape[1]]))


def deal_columns(copy, dealt, given, run):
    copy(
        out=dealt.rearrange("p (t c i) -> p c t i", t=PACK, i=run),
        in_=given.rearrange("p (c i t) -> p c t i", t=PACK, i=run),
    )


def deal_slot(copy, dealt, given, t):
    copy(out=dealt[:, t * P : (t + 1) * P], in_=given[:, t :: PACK])


def tile_list_twotab_agree_one_tabled_kernel(
    tc, xt_words, xt_scales, w_words, w_scales, xo_words, xo_scales, w2_words, w2_scales,
    sg, wb_words, wb_scales, tz, offs, offs2, offs3, offs4, offs5, out,
):
    nc = tc.nc
    with ExitStack() as ctx:
        sb = ctx.enter_context(tc.tile_pool(name="sb", bufs=1))
        psum = ctx.enter_context(tc.psum_pool(name="psum", bufs=1))

        def tile(name, shape, dtype):
            return sb.tile(shape, dtype, name=name, align_bytes=64)

        token_list = tile("token_list", [P, J // 16], U16)
        note_list = tile("note_list", [P, J // 16], U16)
        first_list = tile("first_list", [P, O // 16], U16)
        second_list = tile("second_list", [P, O // 16], U16)
        entry_list = tile("entry_list", [P, O // 16], U16)

        xo_w = tile("xo_w", [P, Z], U16)
        xo_s = tile("xo_s", [P, Z], U8)
        w2_w = tile("w2_w", [P, R], U32)
        w2_s = tile("w2_s", [P, R], U8)
        xt_w = tile("xt_w", [P, T], U32)
        xt_s = tile("xt_s", [P, T], U8)
        w_w = tile("w_w", [P, R], U16)
        w_s = tile("w_s", [P, R], U8)
        wb_w = tile("wb_w", [P, N], U32)
        wb_s = tile("wb_s", [P, N], U8)
        slope = tile("slope", [P, PACK], F32)
        tz_rows = tile("tz_rows", [P, N // P, E], F32)


        load_high_rows(nc.scalar, xo_s, xo_scales)
        load_high_rows(nc.gpsimd, xt_s, xt_scales)
        load_high_rows(nc.gpsimd, w_s, w_scales)
        load_high_rows(nc.gpsimd, wb_s, wb_scales)
        nc.sync.dma_start(note_list[:], offs2)
        nc.sync.dma_start(out=xo_w[:].bitcast(I32), in_=xo_words[0].bitcast(I32))
        load_low_rows(nc.sync, xo_s, xo_scales)
        load_low_rows(nc.sync, w2_s, w2_scales)
        nc.sync.dma_start(out=w2_w[:].bitcast(I32), in_=w2_words[0].rearrange("p n t -> p (n t)").bitcast(I32))
        nc.sync.dma_start(out=w_w[:].bitcast(I32), in_=w_words[0].bitcast(I32))
        load_high_rows(nc.sync, w2_s, w2_scales)
        nc.sync.dma_start(token_list[:], offs)
        load_low_rows(nc.sync, xt_s, xt_scales)
        load_low_rows(nc.sync, w_s, w_scales)
        nc.sync.dma_start(second_list[:], offs4)
        nc.sync.dma_start(out=xt_w[:].bitcast(I32), in_=xt_words[0].rearrange("p n t -> p (n t)").bitcast(I32))
        nc.sync.dma_start(first_list[:], offs3)
        nc.sync.dma_start(out=slope[:], in_=sg.rearrange("(p t) o -> p (t o)", t=PACK))
        nc.sync.dma_start(out=wb_w[:].bitcast(I32), in_=wb_words[0].rearrange("p n t -> p (n t)").bitcast(I32))
        load_low_rows(nc.sync, wb_s, wb_scales)
        nc.sync.dma_start(entry_list[:], offs5)
        nc.sync.dma_start(out=tz_rows[:], in_=tz.rearrange("(h p) e -> p h e", p=P))

        idle = tile("idle", [P, 2], F32)
        nc.vector.memset(idle[:, 0:1], 0.0)
        nc.scalar.activation(out=idle[:, 1:2], in_=idle[:, 0:1], func=ACT.Sigmoid)

        xo_gw = tile("xo_gw", [P, J], U16)
        xo_gs = tile("xo_gs", [P, J], U8)
        w2_dw = tile("w2_dw", [P, R], U32)
        w2_ds = tile("w2_ds", [P, R], U8)
        nc.vector.tensor_copy(xo_gw[:], xo_w[:].indirect(note_list[:]))
        nc.vector.tensor_copy(xo_gs[:], xo_s[:].indirect(note_list[:]))
        deal_columns(nc.scalar.copy, w2_dw[:], w2_w[:], LINE // 4)
        for t in range(PACK):
            deal_slot(nc.vector.tensor_copy, w2_ds, w2_s, t)

        xt_gw = tile("xt_gw", [P, J], U32)
        xt_gs = tile("xt_gs", [P, J], U8)
        w_dw = tile("w2_w", [P, R], U16)
        w_ds = tile("w_ds", [P, R], U8)
        deal_columns(nc.scalar.copy, w_dw[:], w_w[:], LINE // 2)
        nc.vector.tensor_copy(xt_gs[:], xt_s[:].indirect(token_list[:]))
        for t in range(PACK):
            deal_slot(nc.vector.tensor_copy, w_ds, w_s, t)
        nc.vector.tensor_copy(xt_gw[:], xt_w[:].indirect(token_list[:]))

        b_banks = [psum.tile([P, J], F32, name=f"b_bank{t}") for t in range(PACK)]
        for t in range(PACK):
            cols = slice(t * P, (t + 1) * P)
            nc.tensor.matmul_mx(
                out=b_banks[t][:], lhsT=w2_dw[:, cols].bitcast(E5M2), lhsT_scale=w2_ds[:, cols],
                rhs=xo_gw[:].bitcast(E2M1), rhs_scale=xo_gs[:], start=True, stop=True,
            )
        a_banks = [psum.tile([P, J], F32, name=f"a_bank{t}") for t in range(PACK)]
        for t in range(PACK):
            cols = slice(t * P, (t + 1) * P)
            nc.tensor.matmul_mx(
                out=a_banks[t][:], lhsT=w_dw[:, cols].bitcast(E2M1), lhsT_scale=w_ds[:, cols],
                rhs=xt_gw[:].bitcast(E4M3), rhs_scale=xt_gs[:], start=True, stop=True,
            )

        a_rows = [tile(f"a_rows{t}", [P, J], F32) for t in range(PACK)]
        b_rows = [tile(f"b_rows{t}", [P, J], F32) for t in range(PACK)]
        b_first = tile("b_first", [P, PACK, O], F32)
        b_second = tile("b_second", [P, PACK, O], F32)
        gate = tile("gate", [P, PACK, O], F32)
        larger = tile("larger", [P, PACK, O], F32)
        for t in range(PACK):
            nc.scalar.copy(out=b_rows[t][:], in_=b_banks[t][:])
        for t in range(PACK):
            nc.scalar.activation(out=b_second[:, t, :], in_=b_rows[t][:].indirect(second_list[:]), func=ACT.Copy)
        nc.scalar.activation(out=b_first[:, 0, :], in_=b_rows[0][:].indirect(first_list[:]), func=ACT.Copy)
        for t in range(PACK):
            if t > 0:
                nc.vector.tensor_copy(b_first[:, t, :], b_rows[t][:].indirect(first_list[:]))
            nc.vector.tensor_copy(out=a_rows[t][:], in_=a_banks[t][:])
        for t in range(PACK):
            nc.scalar.activation(
                out=gate[:, t, :], in_=a_rows[t][:].indirect(second_list[:]),
                func=ACT.Sigmoid, scale=slope[:, t : t + 1],
            )
        nc.vector.tensor_tensor(out=larger[:], in0=b_first[:], in1=b_second[:], op=ALU.max)

        hid = tile("hid", [P, O * PACK], BF16)
        nc.vector.tensor_tensor(
            out=hid[:].rearrange("p (c i t) -> p c t i", t=PACK, i=4),
            in0=larger[:].rearrange("p t (c i) -> p c t i", i=4),
            in1=gate[:].rearrange("p t (c i) -> p c t i", i=4),
            op=ALU.mult,
        )
        hid_w = tile("hid_w", [P, O], U32)
        hid_s = tile("hid_s", [P, O], U8)
        nc.vector.quantize_mx(out=hid_w[:].bitcast(E4M3), scales=hid_s[:], in_=hid[:])

        tz_picked = tile("a_rows3", [P, N // P, O], F32)
        for h in range(N // P):
            nc.scalar.activation(out=tz_picked[:, h, :], in_=tz_rows[:, h, :].indirect(entry_list[:]), func=ACT.Copy)

        for h in range(N // P):
            cols = slice(h * P, (h + 1) * P)
            p_bank = psum.tile([P, O], F32, name=f"b_bank{h}")
            nc.tensor.matmul_mx(
                out=p_bank[:], lhsT=wb_w[:, cols].bitcast(E5M2), lhsT_scale=wb_s[:, cols],
                rhs=hid_w[:].bitcast(E4M3), rhs_scale=hid_s[:], start=True, stop=True,
            )
            result = tile(f"result{h}", [P, O], F32)
            nc.vector.tensor_tensor(out=result[:], in0=p_bank[:], in1=tz_picked[:, h, :], op=ALU.add)
            nc.sync.dma_start(out=out[cols, :], in_=result[:])
